import numpy as np
import ml_dtypes


def mxq(x, axis, fmt="e4m3"):
    dtype, down = {"e4m3": (ml_dtypes.float8_e4m3fn, 7), "e5m2": (ml_dtypes.float8_e5m2, 14)}[fmt]
    v = np.moveaxis(np.asarray(x, np.float32).astype(ml_dtypes.bfloat16).astype(np.float64), axis, -1)
    blocks = v.reshape(v.shape[:-1] + (-1, 32))
    amax = np.abs(blocks).max(-1, keepdims=True)
    byte = np.maximum(np.where(amax > 0, np.frexp(amax)[1] - 1 + 127, 0) - down, 1)
    scale = np.exp2(byte - 127.0)
    codes = (blocks / scale).astype(np.float32).astype(dtype).astype(np.float64)
    return np.moveaxis((codes * scale).reshape(v.shape), -1, axis)


WIDE = False


def mx_kscale(k):
    if not WIDE:
        return np.ones(k)
    levels = np.array([30, -30])
    if k % 512:
        return np.exp2(np.random.permutation(np.resize(levels, k // 32))).repeat(32)
    a = np.empty((k // 512, 16))
    for p in range(k // 512):
        a[p, :8] = np.random.permutation(np.resize(levels, 8))
        for g in range(8):
            far = levels[np.abs(levels - a[p, g]) >= 10]
            a[p, g + 8] = far[np.random.randint(len(far))]
    return np.exp2(a.ravel()).repeat(32)


def f64(x):
    return np.asarray(x).astype(np.float64)


def striped(idx):
    return np.tile(idx.reshape(-1, 16).T, (8, 1)).astype(np.uint16)


def unstriped(offs):
    return offs[:16].T.reshape(-1).astype(np.int64)


E2M1 = np.array([0.0, 0.5, 1.0, 1.5, 2.0, 3.0, 4.0, 6.0, -0.0, -0.5, -1.0, -1.5, -2.0, -3.0, -4.0, -6.0])


def pack_weight(w, fmt):
    k, n = w.shape
    w = f64(np.asarray(w, np.float32).astype(ml_dtypes.bfloat16)).reshape(k // 32, 32, n)
    amax = np.abs(w).max(1)
    if fmt == "e4m3":
        byte = np.frexp(amax)[1] - 1 + 127 - 7
    else:
        mant, ex = np.frexp(amax / 6.0)
        byte = np.where(mant > 0.5, ex, ex - 1) + 127
    byte = np.clip(np.where(amax > 0, byte, 1), 1, 254)
    scaled = (w * np.exp2(127.0 - byte)[:, None, :]).reshape(k, n).astype(np.float32)
    by_word = np.ascontiguousarray(scaled.reshape(k // 512, 128, 4, n).transpose(0, 1, 3, 2))
    if fmt == "e4m3":
        words = by_word.astype(ml_dtypes.float8_e4m3fn).view(np.uint8)
    else:
        c = by_word.astype(ml_dtypes.float4_e2m1fn).view(np.uint8) & 0xF
        words = (c[..., 0::2] | (c[..., 1::2] << 4)).reshape(k // 512, 128, 2 * n)
    return np.ascontiguousarray(words), np.ascontiguousarray(byte.astype(np.uint8).reshape(k // 512, 16, n))


def unpack_weight(words, scales, fmt):
    g, _, n = scales.shape
    words = np.ascontiguousarray(words).reshape(g, 128, n, -1)
    if fmt == "e4m3":
        vals = words.view(ml_dtypes.float8_e4m3fn).astype(np.float64)
    else:
        nib = np.empty((g, 128, n, 4), np.uint8)
        nib[..., 0::2] = words & 0xF
        nib[..., 1::2] = words >> 4
        vals = E2M1[nib]
    vals = vals * np.repeat(np.exp2(scales.astype(np.float64) - 127.0), 8, axis=1)[..., None]
    return vals.transpose(0, 1, 3, 2).reshape(g * 512, n)


def relu(v):
    return np.maximum(v, 0.0)


def d_relu(v):
    return (v > 0).astype(np.float64)


K, T, E, C, H, N = 256, 1024, 4, 512, 1024, 512


def by_expert(wq, xq):
    return np.concatenate([wq[e].T @ xq[:, e * C:(e + 1) * C] for e in range(E)], axis=1)


def setup_inputs():
    n = np.random.standard_normal
    s = mx_kscale(N)[:, None]
    u = mx_kscale(H)
    first = np.random.permutation(np.repeat(np.arange(E), T // E))
    second = (first + 1 + np.random.permutation(np.repeat(np.arange(E - 1), -(-T // (E - 1)))[:T])) % E
    while np.bincount(second, minlength=E).max() != T // E:
        load = np.bincount(second, minlength=E); hi, lo = int(load.argmax()), int(load.argmin())
        t = np.flatnonzero((second == hi) & (first != lo))[0]; second[t] = lo
    slot_token = np.empty(E * C, np.int64); pos = np.empty((2, T), np.int64); fill = np.zeros(E, np.int64)
    place = np.stack([np.random.permutation(C) for _ in range(E)])
    for r, deal in enumerate((first, second)):
        for t in np.random.permutation(T):
            e = deal[t]; j = e * C + place[e, fill[e]]; fill[e] += 1; slot_token[j] = t; pos[r, t] = j
    g = np.random.uniform(0.2, 0.8, T)
    w_slot = np.empty(E * C); w_slot[pos[0]] = g; w_slot[pos[1]] = 1.0 - g
    w2 = [pack_weight(m, "e2m1") for m in n((E, N, H)) / np.sqrt(N) / s[None] * u[None, None, :]]
    w1 = [pack_weight(m, "e2m1") for m in n((E, H, K)) / np.sqrt(H) / u[None, :, None]]
    w3 = [pack_weight(m, "e2m1") for m in n((E, H, K)) / np.sqrt(H) / u[None, :, None]]
    return {
        "dyT": (n((N, T)) * s).astype(np.float32),
        "a1": n((H, E * C)).astype(np.float32),
        "a3": n((H, E * C)).astype(np.float32),
        "w2_words": np.stack([m[0] for m in w2]),
        "w2_scales": np.stack([m[1] for m in w2]),
        "w1_words": np.stack([m[0] for m in w1]),
        "w1_scales": np.stack([m[1] for m in w1]),
        "w3_words": np.stack([m[0] for m in w3]),
        "w3_scales": np.stack([m[1] for m in w3]),
        "gate": np.tile(w_slot, (N, 1)).astype(np.float32),
        "offs": striped(slot_token),
        "pos1": striped(pos[0]),
        "pos2": striped(pos[1]),
    }


def reference(dyT, a1, a3, w2_words, w2_scales, w1_words, w1_scales, w3_words, w3_scales, gate, offs, pos1, pos2):
    idx = unstriped(offs)
    w2 = np.stack([unpack_weight(w2_words[e], w2_scales[e], "e2m1") for e in range(E)])
    w1 = np.stack([unpack_weight(w1_words[e], w1_scales[e], "e2m1") for e in range(E)])
    w3 = np.stack([unpack_weight(w3_words[e], w3_scales[e], "e2m1") for e in range(E)])
    gq = mxq(f64(gate) * f64(dyT)[:, idx], 0, "e5m2")
    dh = by_expert(w2, gq)
    da1 = dh * f64(a3) * d_relu(f64(a1))
    da3 = dh * relu(f64(a1))
    dx = by_expert(w1, mxq(da1, 0, "e5m2")) + by_expert(w3, mxq(da3, 0, "e5m2"))
    return dx[:, unstriped(pos1)] + dx[:, unstriped(pos2)]

@@ -1,0 +1,264 @@
+from contextlib import ExitStack
+
+import concourse.mybir as mybir
+from concourse.masks import make_identity
+
+K, T, E, C, H, N = 256, 1024, 4, 512, 1024, 512
+S = E * C
+P = 128
+X4 = 4
+NG = H // 512
+SB = C // P
+KB = K // P
+
+F32 = mybir.dt.float32
+BF16 = mybir.dt.bfloat16
+U32 = mybir.dt.uint32
+I32 = mybir.dt.int32
+U16 = mybir.dt.uint16
+U8 = mybir.dt.uint8
+E5M2 = mybir.dt.float8_e5m2_x4
+E2M1 = mybir.dt.float4_e2m1fn_x4
+ALU = mybir.AluOpType
+RELU = mybir.ActivationFunctionType.Relu
+
+FLOPS = 2 * S * N * H + 2 * 2 * S * H * K
+BYTES = 4 * (N * T + 2 * H * S + S + K * T) + E * (N * H + 2 * H * K) // 2 + E * (N * H + 2 * H * K) // 32 + 2 * 128 * 256
+
+
+def by_lines(planes):
+    return planes.rearrange("p t (c i) -> p c t i", i=4)
+
+
+def interleaved(flat):
+    return flat.rearrange("p (c i t) -> p c t i", i=4, t=X4)
+
+
+def tile_moe_bdx_glu_relu_kernel(
+    tc, dyT, a1, a3, w2_words, w2_scales, w1_words, w1_scales, w3_words, w3_scales, gate, offs, pos1, pos2, out
+):
+    nc = tc.nc
+    with ExitStack() as ctx:
+        held = ctx.enter_context(tc.tile_pool(name="held", bufs=1))
+        saved = ctx.enter_context(tc.tile_pool(name="saved", bufs=4))
+        ring = ctx.enter_context(tc.tile_pool(name="ring", bufs=2))
+        turn = ctx.enter_context(tc.tile_pool(name="turn", bufs=8))
+        mid = ctx.enter_context(tc.tile_pool(name="mid", bufs=3))
+        pa = ctx.enter_context(tc.psum_pool(name="pa", bufs=3))
+        pb = ctx.enter_context(tc.psum_pool(name="pb", bufs=3))
+        pc = ctx.enter_context(tc.psum_pool(name="pc", bufs=1))
+
+        offs_sb = held.tile([P, S // 16], U16, name="offs_sb")
+        pos1_sb = held.tile([P, T // 16], U16, name="pos1_sb")
+        pos2_sb = held.tile([P, T // 16], U16, name="pos2_sb")
+        w2_sc = held.tile([P, E, H], U8, name="w2_sc", align_bytes=64)
+        w1_sc = held.tile([P, E * NG, K], U8, name="w1_sc", align_bytes=64)
+        w3_sc = held.tile([P, E * NG, K], U8, name="w3_sc", align_bytes=64)
+        ident = held.tile([P, P], F32, name="ident")
+        nc.vector.memset(w2_sc[:].rearrange("p e i -> p (e i)").bitcast(I32), 0)
+        nc.gpsimd.memset(w1_sc[:].rearrange("p e i -> p (e i)").bitcast(I32), 0)
+        nc.gpsimd.memset(w3_sc[:].rearrange("p e i -> p (e i)").bitcast(I32), 0)
+        make_identity(nc, ident[:])
+
+        nc.sync.dma_start(offs_sb[:], offs)
+        dy_rows = dyT.rearrange("(p t) s -> t p s", t=X4)
+        dy = []
+        gates = []
+        for t in range(X4):
+            dy_t = held.tile([P, T], F32, name=f"dy{t}")
+            nc.sync.dma_start(dy_t[:], dy_rows[t])
+            dy.append(dy_t)
+            if t == 0:
+                gate_0 = held.tile([P, C], F32, name="gate0")
+                nc.sync.dma_start(gate_0[:], gate[0:P, 0:C])
+                gates.append(gate_0)
+
+        w2_w = []
+
+        def load_w2(e):
+            w = held.tile([P, 2 * H], U8, name=f"w2_{e}", align_bytes=64)
+            nc.sync.dma_start(w[:].bitcast(I32), w2_words[e, 0].bitcast(I32))
+            w2_w.append(w)
+
+        def load_scales(plane, scales):
+            by_row = scales.bitcast(I32).rearrange("e s f i -> f (e s) i")
+            for q in range(4):
+                nc.sync.dma_start(plane[32 * q : 32 * q + 4].bitcast(I32), by_row[4 * q : 4 * q + 4])
+
+        a_tiles = {}
+
+        def load_a(e, g):
+            rows = slice(512 * g, 512 * g + 512)
+            cols = slice(C * e, C * e + C)
+            t1 = saved.tile([P, X4, C], F32, name="a1_t")
+            nc.sync.dma_start(t1[:], a1[rows, cols].rearrange("(p t) s -> p t s", t=X4))
+            t3 = saved.tile([P, X4, C], F32, name="a3_t")
+            nc.sync.dma_start(t3[:], a3[rows, cols].rearrange("(p t) s -> p t s", t=X4))
+            a_tiles[e, g] = (t1, t3)
+
+        load_scales(w2_sc, w2_scales)
+        load_w2(0)
+        load_a(0, 0)
+        gate_rest = held.tile([P, S - C], F32, name="gate_rest")
+        nc.sync.dma_start(gate_rest[:], gate[0:P, C:S])
+        load_a(0, 1)
+        load_w2(1)
+        w1_w = held.tile([P, E * NG, 2 * K], U8, name="w1_w", align_bytes=64)
+        nc.sync.dma_start(w1_w[:].bitcast(I32), w1_words.bitcast(I32).rearrange("e s p k -> p (e s) k"))
+        w3_w = held.tile([P, E * NG, 2 * K], U8, name="w3_w", align_bytes=64)
+        nc.sync.dma_start(w3_w[:].bitcast(I32), w3_words.bitcast(I32).rearrange("e s p k -> p (e s) k"))
+        load_scales(w1_sc, w1_scales)
+        load_scales(w3_sc, w3_scales)
+        load_a(1, 0)
+        load_a(1, 1)
+        load_w2(2)
+        load_w2(3)
+        nc.sync.dma_start(pos1_sb[:], pos1)
+        nc.sync.dma_start(pos2_sb[:], pos2)
+
+        dx = [held.tile([P, S], F32, name=f"dx{kb}") for kb in range(KB)]
+
+        g_planes = {}
+        g_codes = {}
+        turned_in = {}
+
+        def gather(e):
+            g4 = ring.tile([P, X4, C], F32, name="g4")
+            gt = gates[0][:] if e == 0 else gate_rest[:, C * (e - 1) : C * e]
+            for t in range(X4):
+                nc.vector.tensor_tensor(
+                    g4[:, t, :], dy[t][:].indirect(offs_sb[:, (C // 16) * e : (C // 16) * (e + 1)]), gt, ALU.mult
+                )
+            g_planes[e] = g4
+
+        def quantise_g(e, step):
+            words = ring.tile([P, C], U32, name="g_words", align_bytes=64)
+            scales = ring.tile([P, C], U8, name="g_scales", align_bytes=64)
+            for s in range(0, C, step):
+                gb = mid.tile([P, X4 * 256], BF16, name="gb", align_bytes=64)
+                run = gb[:, : X4 * step]
+                nc.scalar.copy(interleaved(run), by_lines(g_planes[e][:, :, s : s + step]))
+                nc.vector.quantize_mx(out=words[:, s : s + step].bitcast(E5M2), scales=scales[:, s : s + step], in_=run)
+            g_codes[e] = (words, scales)
+
+        def order(e):
+            if e == 0:
+                return [(g, s) for s in range(SB) for g in range(NG)]
+            return [(g, s) for g in range(NG) for s in range(SB)]
+
+        def first_product(e):
+            words, scales = g_codes[e]
+            for g, s in order(e):
+                bank = pa.tile([P, 512], F32, name="dh_bank")
+                nc.tensor.matmul_mx(
+                    out=bank[:],
+                    lhsT=words[:, P * s : P * s + P].bitcast(E5M2),
+                    lhsT_scale=scales[:, P * s : P * s + P],
+                    rhs=w2_w[e][:, 1024 * g : 1024 * g + 1024].bitcast(E2M1),
+                    rhs_scale=w2_sc[:, e, 512 * g : 512 * g + 512],
+                    start=True,
+                    stop=True,
+                )
+                dht = turn.tile([P, X4, P], F32, name="dht")
+                nc.scalar.copy(dht[:], bank[:].rearrange("p (m t) -> p t m", t=X4))
+                turned_in[e, g, s] = dht
+
+        def relu_a1(e, g):
+            t1 = a_tiles[e, g][0]
+            for t in range(0, X4, 2):
+                nc.scalar.activation(t1[:, t : t + 2, :], t1[:, t : t + 2, :], RELU)
+
+        def hidden(e):
+            d1 = [ring.tile([P, X4 * C], BF16, name=f"d1_{g}", align_bytes=64) for g in range(NG)]
+            d3 = [ring.tile([P, X4 * C], BF16, name=f"d3_{g}", align_bytes=64) for g in range(NG)]
+            held_back = []
+
+            def third(g, s, bank):
+                cols = slice(P * s, P * s + P)
+                run = slice(X4 * P * s, X4 * P * (s + 1))
+                nc.vector.tensor_tensor(
+                    interleaved(d3[g][:, run]), by_lines(bank[:]), by_lines(a_tiles[e, g][0][:, :, cols]), ALU.mult
+                )
+
+            for g, s in order(e):
+                cols = slice(P * s, P * s + P)
+                run = slice(X4 * P * s, X4 * P * (s + 1))
+                dht = turned_in[e, g, s]
+                bank = pb.tile([P, X4, P], F32, name="turned")
+                for t in range(X4):
+                    nc.tensor.transpose(bank[:, t, :], dht[:, t, :], ident[:])
+                masked = mid.tile([P, X4, P], F32, name="masked")
+                nc.vector.scalar_tensor_tensor(
+                    masked[:], a_tiles[e, g][0][:, :, cols], 0.0, bank[:], ALU.is_gt, ALU.mult
+                )
+                nc.gpsimd.tensor_tensor(
+                    interleaved(d1[g][:, run]), by_lines(masked[:]), by_lines(a_tiles[e, g][1][:, :, cols]), ALU.mult
+                )
+                held_back.append((g, s, bank))
+                if len(held_back) > 1:
+                    third(*held_back.pop(0))
+            third(*held_back.pop(0))
+            return d1, d3
+
+        def quantise_hidden(e, d1, d3):
+            codes = {}
+            for which, d in ((3, d3), (1, d1)):
+                for g in range(NG):
+                    words = ring.tile([P, C], U32, name=f"d_words{which}{g}", align_bytes=64)
+                    scales = ring.tile([P, C], U8, name=f"d_scales{which}{g}", align_bytes=64)
+                    nc.vector.quantize_mx(out=words[:].bitcast(E5M2), scales=scales[:], in_=d[g][:])
+                    codes[which, g] = (words, scales)
+            return codes
+
+        def second_product(e, codes):
+            for kb in range(KB):
+                bank = pc.tile([P, C], F32, name=f"dx_bank{kb}")
+                passes = [(which, g) for which in (3, 1) for g in range(NG)]
+                for n, (which, g) in enumerate(passes):
+                    w, sc = (w1_w, w1_sc) if which == 1 else (w3_w, w3_sc)
+                    words, scales = codes[which, g]
+                    nc.tensor.matmul_mx(
+                        out=bank[:],
+                        lhsT=w[:, NG * e + g, 2 * P * kb : 2 * P * (kb + 1)].bitcast(E2M1),
+                        lhsT_scale=sc[:, NG * e + g, P * kb : P * (kb + 1)],
+                        rhs=words[:].bitcast(E5M2),
+                        rhs_scale=scales[:],
+                        start=(n == 0),
+                        stop=(n == len(passes) - 1),
+                    )
+                nc.scalar.copy(dx[kb][:, C * e : C * (e + 1)], bank[:])
+
+        gather(0)
+        quantise_g(0, 128)
+        first_product(0)
+        gather(1)
+        relu_a1(0, 0)
+        relu_a1(0, 1)
+        for e in range(E):
+            d1, d3 = hidden(e)
+            if e + 1 < E:
+                quantise_g(e + 1, 256)
+                first_product(e + 1)
+                relu_a1(e + 1, 0)
+                relu_a1(e + 1, 1)
+            codes = quantise_hidden(e, d1, d3)
+            if e + 2 < E:
+                load_a(e + 2, 0)
+                load_a(e + 2, 1)
+                gather(e + 2)
+            second_product(e, codes)
+
+        for kb in range(KB):
+            half = T // (kb + 1)
+            picks = ring.tile([P, X4, C], F32, name="g4")
+            flat = picks[:].rearrange("p t c -> p (t c)")
+            first, second = flat[:, 0:T], flat[:, T : 2 * T]
+            total = ring.tile([P, T], F32, name="total")
+            for h in range(0, T, half):
+                span = slice(h, h + half)
+                lists = slice(h // 16, (h + half) // 16)
+                nc.vector.tensor_copy(first[:, span], dx[kb][:].indirect(pos1_sb[:, lists]))
+                nc.vector.tensor_copy(second[:, span], dx[kb][:].indirect(pos2_sb[:, lists]))
+                engine = nc.gpsimd if kb == 0 else nc.vector
+                engine.tensor_tensor(total[:, span], first[:, span], second[:, span], ALU.add)
+                nc.sync.dma_start(out[P * kb : P * (kb + 1), span], total[:, span])

@@ -30,6 +30,14 @@ def by_lines(planes):
     return planes.rearrange("p t (c i) -> p c t i", i=4)
 
 
+def by_column(flat):
+    return flat.rearrange("p (j t) -> p j t", t=X4)
+
+
+def across(bank):
+    return bank[:].rearrange("p t j -> p j t")
+
+
 def interleaved(flat):
     return flat.rearrange("p (c i t) -> p c t i", i=4, t=X4)
 
@@ -55,23 +63,26 @@ def tile_moe_bdx_glu_relu_kernel(
         w1_sc = held.tile([P, E * NG, K], U8, name="w1_sc", align_bytes=64)
         w3_sc = held.tile([P, E * NG, K], U8, name="w3_sc", align_bytes=64)
         ident = held.tile([P, P], F32, name="ident")
-        nc.vector.memset(w2_sc[:].rearrange("p e i -> p (e i)").bitcast(I32), 0)
-        nc.gpsimd.memset(w1_sc[:].rearrange("p e i -> p (e i)").bitcast(I32), 0)
-        nc.gpsimd.memset(w3_sc[:].rearrange("p e i -> p (e i)").bitcast(I32), 0)
+        for plane in (w2_sc, w1_sc, w3_sc):
+            nc.vector.memset(plane[:].rearrange("p e i -> p (e i)").bitcast(I32), 0)
         make_identity(nc, ident[:])
 
         nc.sync.dma_start(offs_sb[:], offs)
         dy_rows = dyT.rearrange("(p t) s -> t p s", t=X4)
         dy = []
         gates = []
+
+        def load_gate(e):
+            gate_e = held.tile([P, C], F32, name=f"gate{e}")
+            nc.sync.dma_start(gate_e[:], gate[0:P, C * e : C * (e + 1)])
+            gates.append(gate_e)
+
         for t in range(X4):
             dy_t = held.tile([P, T], F32, name=f"dy{t}")
             nc.sync.dma_start(dy_t[:], dy_rows[t])
             dy.append(dy_t)
             if t == 0:
-                gate_0 = held.tile([P, C], F32, name="gate0")
-                nc.sync.dma_start(gate_0[:], gate[0:P, 0:C])
-                gates.append(gate_0)
+                load_gate(0)
 
         w2_w = []
 
@@ -80,37 +91,39 @@ def tile_moe_bdx_glu_relu_kernel(
             nc.sync.dma_start(w[:].bitcast(I32), w2_words[e, 0].bitcast(I32))
             w2_w.append(w)
 
-        def load_scales(plane, scales):
+        def load_scales(queue, plane, scales):
             by_row = scales.bitcast(I32).rearrange("e s f i -> f (e s) i")
             for q in range(4):
-                nc.sync.dma_start(plane[32 * q : 32 * q + 4].bitcast(I32), by_row[4 * q : 4 * q + 4])
+                queue.dma_start(plane[32 * q : 32 * q + 4].bitcast(I32), by_row[4 * q : 4 * q + 4])
 
         a_tiles = {}
 
-        def load_a(e, g):
+        def load_a(which, e, g):
             rows = slice(512 * g, 512 * g + 512)
             cols = slice(C * e, C * e + C)
-            t1 = saved.tile([P, X4, C], F32, name="a1_t")
-            nc.sync.dma_start(t1[:], a1[rows, cols].rearrange("(p t) s -> p t s", t=X4))
-            t3 = saved.tile([P, X4, C], F32, name="a3_t")
-            nc.sync.dma_start(t3[:], a3[rows, cols].rearrange("(p t) s -> p t s", t=X4))
-            a_tiles[e, g] = (t1, t3)
+            tile_a = saved.tile([P, X4, C], F32, name=f"a{which}_t", bufs=2 if which == 1 else 4)
+            nc.sync.dma_start(tile_a[:], (a1 if which == 1 else a3)[rows, cols].rearrange("(p t) s -> p t s", t=X4))
+            a_tiles[which, e, g] = tile_a
 
-        load_scales(w2_sc, w2_scales)
+        load_scales(nc.sync, w2_sc, w2_scales)
+        load_scales(nc.gpsimd, w1_sc, w1_scales)
+        load_scales(nc.gpsimd, w3_sc, w3_scales)
         load_w2(0)
-        load_a(0, 0)
-        gate_rest = held.tile([P, S - C], F32, name="gate_rest")
-        nc.sync.dma_start(gate_rest[:], gate[0:P, C:S])
-        load_a(0, 1)
+        load_a(1, 0, 0)
+        load_gate(1)
+        load_a(1, 0, 1)
+        load_a(3, 0, 0)
         load_w2(1)
+        load_a(3, 0, 1)
+        load_gate(2)
+        load_gate(3)
         w1_w = held.tile([P, E * NG, 2 * K], U8, name="w1_w", align_bytes=64)
         nc.sync.dma_start(w1_w[:].bitcast(I32), w1_words.bitcast(I32).rearrange("e s p k -> p (e s) k"))
         w3_w = held.tile([P, E * NG, 2 * K], U8, name="w3_w", align_bytes=64)
         nc.sync.dma_start(w3_w[:].bitcast(I32), w3_words.bitcast(I32).rearrange("e s p k -> p (e s) k"))
-        load_scales(w1_sc, w1_scales)
-        load_scales(w3_sc, w3_scales)
-        load_a(1, 0)
-        load_a(1, 1)
+        for g in range(NG):
+            load_a(1, 1, g)
+            load_a(3, 1, g)
         load_w2(2)
         load_w2(3)
         nc.sync.dma_start(pos1_sb[:], pos1)
@@ -121,13 +134,13 @@ def tile_moe_bdx_glu_relu_kernel(
         g_planes = {}
         g_codes = {}
         turned_in = {}
+        relu_a1 = {}
 
         def gather(e):
             g4 = ring.tile([P, X4, C], F32, name="g4")
-            gt = gates[0][:] if e == 0 else gate_rest[:, C * (e - 1) : C * e]
             for t in range(X4):
                 nc.vector.tensor_tensor(
-                    g4[:, t, :], dy[t][:].indirect(offs_sb[:, (C // 16) * e : (C // 16) * (e + 1)]), gt, ALU.mult
+                    g4[:, t, :], dy[t][:].indirect(offs_sb[:, (C // 16) * e : (C // 16) * (e + 1)]), gates[e][:], ALU.mult
                 )
             g_planes[e] = g4
 
@@ -135,20 +148,17 @@ def tile_moe_bdx_glu_relu_kernel(
             words = ring.tile([P, C], U32, name="g_words", align_bytes=64)
             scales = ring.tile([P, C], U8, name="g_scales", align_bytes=64)
             for s in range(0, C, step):
-                gb = mid.tile([P, X4 * 256], BF16, name="gb", align_bytes=64)
+                gb = mid.tile([P, X4 * 256], BF16, name="gb", align_bytes=64, bufs=2)
                 run = gb[:, : X4 * step]
                 nc.scalar.copy(interleaved(run), by_lines(g_planes[e][:, :, s : s + step]))
                 nc.vector.quantize_mx(out=words[:, s : s + step].bitcast(E5M2), scales=scales[:, s : s + step], in_=run)
             g_codes[e] = (words, scales)
 
-        def order(e):
-            if e == 0:
-                return [(g, s) for s in range(SB) for g in range(NG)]
-            return [(g, s) for g in range(NG) for s in range(SB)]
+        order = [(g, s) for g in range(NG) for s in range(SB)]
 
         def first_product(e):
             words, scales = g_codes[e]
-            for g, s in order(e):
+            for g, s in order:
                 bank = pa.tile([P, 512], F32, name="dh_bank")
                 nc.tensor.matmul_mx(
                     out=bank[:],
@@ -162,61 +172,66 @@ def tile_moe_bdx_glu_relu_kernel(
                 dht = turn.tile([P, X4, P], F32, name="dht")
                 nc.scalar.copy(dht[:], bank[:].rearrange("p (m t) -> p t m", t=X4))
                 turned_in[e, g, s] = dht
+                if s == 0:
+                    relu_a1[e, g] = saved.tile([P, X4 * C], F32, name="relu_a1", bufs=3)
+                nc.scalar.activation(
+                    relu_a1[e, g][:, X4 * P * s : X4 * P * (s + 1)].rearrange("p (j t) -> p j t", t=X4),
+                    a_tiles[1, e, g][:, :, P * s : P * (s + 1)].rearrange("p t j -> p j t"),
+                    RELU,
+                )
 
-        def relu_a1(e, g):
-            t1 = a_tiles[e, g][0]
-            for t in range(0, X4, 2):
-                nc.scalar.activation(t1[:, t : t + 2, :], t1[:, t : t + 2, :], RELU)
-
-        def hidden(e):
+        def hidden(e, between):
             d1 = [ring.tile([P, X4 * C], BF16, name=f"d1_{g}", align_bytes=64) for g in range(NG)]
-            d3 = [ring.tile([P, X4 * C], BF16, name=f"d3_{g}", align_bytes=64) for g in range(NG)]
+            d3 = [ring.tile([P, X4 * C], BF16, name=f"d3_{g}", align_bytes=64, bufs=1) for g in range(NG)]
             held_back = []
 
             def third(g, s, bank):
-                cols = slice(P * s, P * s + P)
                 run = slice(X4 * P * s, X4 * P * (s + 1))
-                nc.vector.tensor_tensor(
-                    interleaved(d3[g][:, run]), by_lines(bank[:]), by_lines(a_tiles[e, g][0][:, :, cols]), ALU.mult
-                )
+                nc.vector.tensor_tensor(by_column(d3[g][:, run]), across(bank), by_column(relu_a1[e, g][:, run]), ALU.mult)
 
-            for g, s in order(e):
-                cols = slice(P * s, P * s + P)
-                run = slice(X4 * P * s, X4 * P * (s + 1))
+            for n, (g, s) in enumerate(order):
                 dht = turned_in[e, g, s]
                 bank = pb.tile([P, X4, P], F32, name="turned")
                 for t in range(X4):
                     nc.tensor.transpose(bank[:, t, :], dht[:, t, :], ident[:])
-                masked = mid.tile([P, X4, P], F32, name="masked")
+                if n % 2 == 0:
+                    masked = mid.tile([P, X4 * 2 * P], F32, name="masked")
+                run = slice(X4 * P * s, X4 * P * (s + 1))
+                half = slice(X4 * P * (n % 2), X4 * P * (n % 2 + 1))
                 nc.vector.scalar_tensor_tensor(
-                    masked[:], a_tiles[e, g][0][:, :, cols], 0.0, bank[:], ALU.is_gt, ALU.mult
+                    by_column(masked[:, half]), by_column(relu_a1[e, g][:, run]), 0.0, across(bank), ALU.is_gt, ALU.mult
                 )
-                nc.gpsimd.tensor_tensor(
-                    interleaved(d1[g][:, run]), by_lines(masked[:]), by_lines(a_tiles[e, g][1][:, :, cols]), ALU.mult
-                )
+                if n % 2 == 1:
+                    pair = slice(P * (s - 1), P * (s + 1))
+                    engine = nc.vector if (e >= 2 and n == 7) else nc.gpsimd
+                    engine.tensor_tensor(
+                        by_column(d1[g][:, X4 * P * (s - 1) : X4 * P * (s + 1)]),
+                        by_column(masked[:]),
+                        a_tiles[3, e, g][:, :, pair].rearrange("p t j -> p j t"),
+                        ALU.mult,
+                    )
                 held_back.append((g, s, bank))
                 if len(held_back) > 1:
                     third(*held_back.pop(0))
+                between(n)
             third(*held_back.pop(0))
             return d1, d3
 
-        def quantise_hidden(e, d1, d3):
-            codes = {}
-            for which, d in ((3, d3), (1, d1)):
-                for g in range(NG):
-                    words = ring.tile([P, C], U32, name=f"d_words{which}{g}", align_bytes=64)
-                    scales = ring.tile([P, C], U8, name=f"d_scales{which}{g}", align_bytes=64)
-                    nc.vector.quantize_mx(out=words[:].bitcast(E5M2), scales=scales[:], in_=d[g][:])
-                    codes[which, g] = (words, scales)
-            return codes
+        codes = {}
 
-        def second_product(e, codes):
+        def quantise_hidden(which, e, g, d):
+            words = ring.tile([P, C], U32, name=f"d_words{which}{g}", align_bytes=64)
+            scales = ring.tile([P, C], U8, name=f"d_scales{which}{g}", align_bytes=64)
+            nc.vector.quantize_mx(out=words[:].bitcast(E5M2), scales=scales[:], in_=d[g][:])
+            codes[which, e, g] = (words, scales)
+
+        def second_product(e):
             for kb in range(KB):
                 bank = pc.tile([P, C], F32, name=f"dx_bank{kb}")
                 passes = [(which, g) for which in (3, 1) for g in range(NG)]
                 for n, (which, g) in enumerate(passes):
                     w, sc = (w1_w, w1_sc) if which == 1 else (w3_w, w3_sc)
-                    words, scales = codes[which, g]
+                    words, scales = codes[which, e, g]
                     nc.tensor.matmul_mx(
                         out=bank[:],
                         lhsT=w[:, NG * e + g, 2 * P * kb : 2 * P * (kb + 1)].bitcast(E2M1),
@@ -232,28 +247,37 @@ def tile_moe_bdx_glu_relu_kernel(
         quantise_g(0, 128)
         first_product(0)
         gather(1)
-        relu_a1(0, 0)
-        relu_a1(0, 1)
+        before = {}
         for e in range(E):
-            d1, d3 = hidden(e)
-            if e + 1 < E:
-                quantise_g(e + 1, 256)
-                first_product(e + 1)
-                relu_a1(e + 1, 0)
-                relu_a1(e + 1, 1)
-            codes = quantise_hidden(e, d1, d3)
+
+            def between(n):
+                if n == 1 and e + 1 < E:
+                    quantise_g(e + 1, 256)
+                    first_product(e + 1)
+                if n == 3 and e > 0:
+                    for g in range(NG):
+                        quantise_hidden(1, e - 1, g, before["d1"])
+                    second_product(e - 1)
+
+            d1, d3 = hidden(e, between)
+            before["d1"] = d1
+            for g in range(NG):
+                quantise_hidden(3, e, g, d3)
             if e + 2 < E:
-                load_a(e + 2, 0)
-                load_a(e + 2, 1)
+                for g in range(NG):
+                    load_a(1, e + 2, g)
+                    load_a(3, e + 2, g)
                 gather(e + 2)
-            second_product(e, codes)
+        for g in range(NG):
+            quantise_hidden(1, E - 1, g, before["d1"])
+        second_product(E - 1)
 
         for kb in range(KB):
             half = T // (kb + 1)
             picks = ring.tile([P, X4, C], F32, name="g4")
             flat = picks[:].rearrange("p t c -> p (t c)")
             first, second = flat[:, 0:T], flat[:, T : 2 * T]
-            total = ring.tile([P, T], F32, name="total")
+            total = ring.tile([P, T], F32, name="total", bufs=1)
             for h in range(0, T, half):
                 span = slice(h, h + half)
                 lists = slice(h // 16, (h + half) // 16)

@@ -20,7 +20,7 @@ U8 = mybir.dt.uint8
 E5M2 = mybir.dt.float8_e5m2_x4
 E2M1 = mybir.dt.float4_e2m1fn_x4
 ALU = mybir.AluOpType
-RELU = mybir.ActivationFunctionType.Relu
+ACT = mybir.ActivationFunctionType
 
 FLOPS = 2 * S * N * H + 2 * 2 * S * H * K
 BYTES = 4 * (N * T + 2 * H * S + S + K * T) + E * (N * H + 2 * H * K) // 2 + E * (N * H + 2 * H * K) // 32 + 2 * 128 * 256
@@ -28,14 +28,6 @@ BYTES = 4 * (N * T + 2 * H * S + S + K * T) + E * (N * H + 2 * H * K) // 2 + E *
 
 def by_lines(planes):
     return planes.rearrange("p t (c i) -> p c t i", i=4)
-
-
-def by_column(flat):
-    return flat.rearrange("p (j t) -> p j t", t=X4)
-
-
-def across(bank):
-    return bank[:].rearrange("p t j -> p j t")
 
 
 def interleaved(flat):
@@ -101,13 +93,11 @@ def tile_moe_bdx_glu_relu_kernel(
         def load_a(which, e, g):
             rows = slice(512 * g, 512 * g + 512)
             cols = slice(C * e, C * e + C)
-            tile_a = saved.tile([P, X4, C], F32, name=f"a{which}_t", bufs=2 if which == 1 else 4)
+            tile_a = saved.tile([P, X4, C], F32, name=f"a{which}_t")
             nc.sync.dma_start(tile_a[:], (a1 if which == 1 else a3)[rows, cols].rearrange("(p t) s -> p t s", t=X4))
             a_tiles[which, e, g] = tile_a
 
         load_scales(nc.sync, w2_sc, w2_scales)
-        load_scales(nc.gpsimd, w1_sc, w1_scales)
-        load_scales(nc.gpsimd, w3_sc, w3_scales)
         load_w2(0)
         load_a(1, 0, 0)
         load_gate(1)
@@ -115,6 +105,8 @@ def tile_moe_bdx_glu_relu_kernel(
         load_a(3, 0, 0)
         load_w2(1)
         load_a(3, 0, 1)
+        load_scales(nc.sync, w1_sc, w1_scales)
+        load_scales(nc.sync, w3_sc, w3_scales)
         load_gate(2)
         load_gate(3)
         w1_w = held.tile([P, E * NG, 2 * K], U8, name="w1_w", align_bytes=64)
@@ -134,7 +126,7 @@ def tile_moe_bdx_glu_relu_kernel(
         g_planes = {}
         g_codes = {}
         turned_in = {}
-        relu_a1 = {}
+        steps_1 = {}
 
         def gather(e):
             g4 = ring.tile([P, X4, C], F32, name="g4")
@@ -172,63 +164,47 @@ def tile_moe_bdx_glu_relu_kernel(
                 dht = turn.tile([P, X4, P], F32, name="dht")
                 nc.scalar.copy(dht[:], bank[:].rearrange("p (m t) -> p t m", t=X4))
                 turned_in[e, g, s] = dht
+                kept = a_tiles[1, e, g][:, :, P * s : P * (s + 1)]
+                nc.scalar.activation(kept, kept, ACT.Relu)
                 if s == 0:
-                    relu_a1[e, g] = saved.tile([P, X4 * C], F32, name="relu_a1", bufs=3)
+                    steps_1[e, g] = ring.tile([P, X4 * C], BF16, name="mask", bufs=3, align_bytes=64)
                 nc.scalar.activation(
-                    relu_a1[e, g][:, X4 * P * s : X4 * P * (s + 1)].rearrange("p (j t) -> p j t", t=X4),
-                    a_tiles[1, e, g][:, :, P * s : P * (s + 1)].rearrange("p t j -> p j t"),
-                    RELU,
+                    interleaved(steps_1[e, g][:, X4 * P * s : X4 * P * (s + 1)]), by_lines(kept), ACT.Sign
                 )
 
         def hidden(e, between):
-            d1 = [ring.tile([P, X4 * C], BF16, name=f"d1_{g}", align_bytes=64) for g in range(NG)]
+            d1 = [ring.tile([P, X4 * C], BF16, name=f"d1_{g}", align_bytes=64, bufs=1) for g in range(NG)]
             d3 = [ring.tile([P, X4 * C], BF16, name=f"d3_{g}", align_bytes=64, bufs=1) for g in range(NG)]
-            held_back = []
-
-            def third(g, s, bank):
-                run = slice(X4 * P * s, X4 * P * (s + 1))
-                nc.vector.tensor_tensor(by_column(d3[g][:, run]), across(bank), by_column(relu_a1[e, g][:, run]), ALU.mult)
-
             for n, (g, s) in enumerate(order):
+                cols = slice(P * s, P * s + P)
+                run = slice(X4 * P * s, X4 * P * (s + 1))
                 dht = turned_in[e, g, s]
                 bank = pb.tile([P, X4, P], F32, name="turned")
                 for t in range(X4):
                     nc.tensor.transpose(bank[:, t, :], dht[:, t, :], ident[:])
-                if n % 2 == 0:
-                    masked = mid.tile([P, X4 * 2 * P], F32, name="masked")
-                run = slice(X4 * P * s, X4 * P * (s + 1))
-                half = slice(X4 * P * (n % 2), X4 * P * (n % 2 + 1))
-                nc.vector.scalar_tensor_tensor(
-                    by_column(masked[:, half]), by_column(relu_a1[e, g][:, run]), 0.0, across(bank), ALU.is_gt, ALU.mult
-                )
-                if n % 2 == 1:
-                    pair = slice(P * (s - 1), P * (s + 1))
-                    engine = nc.vector if (e >= 2 and n == 7) else nc.gpsimd
-                    engine.tensor_tensor(
-                        by_column(d1[g][:, X4 * P * (s - 1) : X4 * P * (s + 1)]),
-                        by_column(masked[:]),
-                        a_tiles[3, e, g][:, :, pair].rearrange("p t j -> p j t"),
-                        ALU.mult,
+                for d, which in ((d3, 1), (d1, 3)):
+                    nc.vector.tensor_tensor(
+                        interleaved(d[g][:, run]), by_lines(bank[:]), by_lines(a_tiles[which, e, g][:, :, cols]), ALU.mult
                     )
-                held_back.append((g, s, bank))
-                if len(held_back) > 1:
-                    third(*held_back.pop(0))
-                between(n)
-            third(*held_back.pop(0))
-            return d1, d3
+                between(n, d1, d3)
 
         codes = {}
+
+        def close_half(e, g, d1, d3):
+            nc.vector.tensor_tensor(d1[g][:], d1[g][:], steps_1[e, g][:], ALU.mult)
+            quantise_hidden(3, e, g, d3[g])
+            quantise_hidden(1, e, g, d1[g])
 
         def quantise_hidden(which, e, g, d):
             words = ring.tile([P, C], U32, name=f"d_words{which}{g}", align_bytes=64)
             scales = ring.tile([P, C], U8, name=f"d_scales{which}{g}", align_bytes=64)
-            nc.vector.quantize_mx(out=words[:].bitcast(E5M2), scales=scales[:], in_=d[g][:])
+            nc.vector.quantize_mx(out=words[:].bitcast(E5M2), scales=scales[:], in_=d[:])
             codes[which, e, g] = (words, scales)
 
         def second_product(e):
             for kb in range(KB):
                 bank = pc.tile([P, C], F32, name=f"dx_bank{kb}")
-                passes = [(which, g) for which in (3, 1) for g in range(NG)]
+                passes = [(which, g) for g in range(NG) for which in (3, 1)]
                 for n, (which, g) in enumerate(passes):
                     w, sc = (w1_w, w1_sc) if which == 1 else (w3_w, w3_sc)
                     words, scales = codes[which, e, g]
@@ -247,30 +223,24 @@ def tile_moe_bdx_glu_relu_kernel(
         quantise_g(0, 128)
         first_product(0)
         gather(1)
-        before = {}
         for e in range(E):
 
-            def between(n):
+            def between(n, d1, d3):
                 if n == 1 and e + 1 < E:
                     quantise_g(e + 1, 256)
                     first_product(e + 1)
-                if n == 3 and e > 0:
-                    for g in range(NG):
-                        quantise_hidden(1, e - 1, g, before["d1"])
-                    second_product(e - 1)
+                if n == 4:
+                    close_half(e, 0, d1, d3)
+                if n == 7:
+                    close_half(e, 1, d1, d3)
 
-            d1, d3 = hidden(e, between)
-            before["d1"] = d1
-            for g in range(NG):
-                quantise_hidden(3, e, g, d3)
+            hidden(e, between)
             if e + 2 < E:
                 for g in range(NG):
                     load_a(1, e + 2, g)
                     load_a(3, e + 2, g)
                 gather(e + 2)
-        for g in range(NG):
-            quantise_hidden(1, E - 1, g, before["d1"])
-        second_product(E - 1)
+            second_product(e)
 
         for kb in range(KB):
             half = T // (kb + 1)

@@ -166,11 +166,9 @@ def tile_moe_bdx_glu_relu_kernel(
                 turned_in[e, g, s] = dht
                 kept = a_tiles[1, e, g][:, :, P * s : P * (s + 1)]
                 nc.scalar.activation(kept, kept, ACT.Relu)
-                if s == 0:
+                if s == SB - 1:
                     steps_1[e, g] = ring.tile([P, X4 * C], BF16, name="mask", bufs=3, align_bytes=64)
-                nc.scalar.activation(
-                    interleaved(steps_1[e, g][:, X4 * P * s : X4 * P * (s + 1)]), by_lines(kept), ACT.Sign
-                )
+                    nc.scalar.activation(interleaved(steps_1[e, g][:]), by_lines(a_tiles[1, e, g][:]), ACT.Sign)
 
         def hidden(e, between):
             d1 = [ring.tile([P, X4 * C], BF16, name=f"d1_{g}", align_bytes=64, bufs=1) for g in range(NG)]

from contextlib import ExitStack

import concourse.mybir as mybir
from concourse.masks import make_identity

K, T, E, C, H, N = 256, 1024, 4, 512, 1024, 512
S = E * C
P = 128
X4 = 4
NG = H // 512
SB = C // P
KB = K // P

F32 = mybir.dt.float32
BF16 = mybir.dt.bfloat16
U32 = mybir.dt.uint32
I32 = mybir.dt.int32
U16 = mybir.dt.uint16
U8 = mybir.dt.uint8
E5M2 = mybir.dt.float8_e5m2_x4
E2M1 = mybir.dt.float4_e2m1fn_x4
ALU = mybir.AluOpType
ACT = mybir.ActivationFunctionType

FLOPS = 2 * S * N * H + 2 * 2 * S * H * K
BYTES = 4 * (N * T + 2 * H * S + S + K * T) + E * (N * H + 2 * H * K) // 2 + E * (N * H + 2 * H * K) // 32 + 2 * 128 * 256


def by_lines(planes):
    return planes.rearrange("p t (c i) -> p c t i", i=4)


def interleaved(flat):
    return flat.rearrange("p (c i t) -> p c t i", i=4, t=X4)


def tile_moe_bdx_glu_relu_kernel(
    tc, dyT, a1, a3, w2_words, w2_scales, w1_words, w1_scales, w3_words, w3_scales, gate, offs, pos1, pos2, out
):
    nc = tc.nc
    with ExitStack() as ctx:
        held = ctx.enter_context(tc.tile_pool(name="held", bufs=1))
        saved = ctx.enter_context(tc.tile_pool(name="saved", bufs=4))
        ring = ctx.enter_context(tc.tile_pool(name="ring", bufs=2))
        turn = ctx.enter_context(tc.tile_pool(name="turn", bufs=8))
        mid = ctx.enter_context(tc.tile_pool(name="mid", bufs=3))
        pa = ctx.enter_context(tc.psum_pool(name="pa", bufs=3))
        pb = ctx.enter_context(tc.psum_pool(name="pb", bufs=3))
        pc = ctx.enter_context(tc.psum_pool(name="pc", bufs=1))

        offs_sb = held.tile([P, S // 16], U16, name="offs_sb")
        pos1_sb = held.tile([P, T // 16], U16, name="pos1_sb")
        pos2_sb = held.tile([P, T // 16], U16, name="pos2_sb")
        w2_sc = held.tile([P, E, H], U8, name="w2_sc", align_bytes=64)
        w1_sc = held.tile([P, E * NG, K], U8, name="w1_sc", align_bytes=64)
        w3_sc = held.tile([P, E * NG, K], U8, name="w3_sc", align_bytes=64)
        ident = held.tile([P, P], F32, name="ident")
        for plane in (w2_sc, w1_sc, w3_sc):
            nc.vector.memset(plane[:].rearrange("p e i -> p (e i)").bitcast(I32), 0)
        make_identity(nc, ident[:])

        nc.sync.dma_start(offs_sb[:], offs)
        dy_rows = dyT.rearrange("(p t) s -> t p s", t=X4)
        dy = []
        gates = []

        def load_gate(e):
            gate_e = held.tile([P, C], F32, name=f"gate{e}")
            nc.sync.dma_start(gate_e[:], gate[0:P, C * e : C * (e + 1)])
            gates.append(gate_e)

        for t in range(X4):
            dy_t = held.tile([P, T], F32, name=f"dy{t}")
            nc.sync.dma_start(dy_t[:], dy_rows[t])
            dy.append(dy_t)
            if t == 0:
                load_gate(0)

        w2_w = []

        def load_w2(e):
            w = held.tile([P, 2 * H], U8, name=f"w2_{e}", align_bytes=64)
            nc.sync.dma_start(w[:].bitcast(I32), w2_words[e, 0].bitcast(I32))
            w2_w.append(w)

        def load_scales(queue, plane, scales):
            by_row = scales.bitcast(I32).rearrange("e s f i -> f (e s) i")
            for q in range(4):
                queue.dma_start(plane[32 * q : 32 * q + 4].bitcast(I32), by_row[4 * q : 4 * q + 4])

        a_tiles = {}

        def load_a(which, e, g):
            rows = slice(512 * g, 512 * g + 512)
            cols = slice(C * e, C * e + C)
            tile_a = saved.tile([P, X4, C], F32, name=f"a{which}_t")
            nc.sync.dma_start(tile_a[:], (a1 if which == 1 else a3)[rows, cols].rearrange("(p t) s -> p t s", t=X4))
            a_tiles[which, e, g] = tile_a

        load_scales(nc.sync, w2_sc, w2_scales)
        load_w2(0)
        load_a(1, 0, 0)
        load_gate(1)
        load_a(1, 0, 1)
        load_a(3, 0, 0)
        load_w2(1)
        load_a(3, 0, 1)
        load_scales(nc.sync, w1_sc, w1_scales)
        load_scales(nc.sync, w3_sc, w3_scales)
        load_gate(2)
        load_gate(3)
        w1_w = held.tile([P, E * NG, 2 * K], U8, name="w1_w", align_bytes=64)
        nc.sync.dma_start(w1_w[:].bitcast(I32), w1_words.bitcast(I32).rearrange("e s p k -> p (e s) k"))
        w3_w = held.tile([P, E * NG, 2 * K], U8, name="w3_w", align_bytes=64)
        nc.sync.dma_start(w3_w[:].bitcast(I32), w3_words.bitcast(I32).rearrange("e s p k -> p (e s) k"))
        for g in range(NG):
            load_a(1, 1, g)
            load_a(3, 1, g)
        load_w2(2)
        load_w2(3)
        nc.sync.dma_start(pos1_sb[:], pos1)
        nc.sync.dma_start(pos2_sb[:], pos2)

        dx = [held.tile([P, S], F32, name=f"dx{kb}") for kb in range(KB)]

        g_planes = {}
        g_codes = {}
        turned_in = {}
        steps_1 = {}

        def gather(e):
            g4 = ring.tile([P, X4, C], F32, name="g4")
            for t in range(X4):
                nc.vector.tensor_tensor(
                    g4[:, t, :], dy[t][:].indirect(offs_sb[:, (C // 16) * e : (C // 16) * (e + 1)]), gates[e][:], ALU.mult
                )
            g_planes[e] = g4

        def quantise_g(e, step):
            words = ring.tile([P, C], U32, name="g_words", align_bytes=64)
            scales = ring.tile([P, C], U8, name="g_scales", align_bytes=64)
            for s in range(0, C, step):
                gb = mid.tile([P, X4 * 256], BF16, name="gb", align_bytes=64, bufs=2)
                run = gb[:, : X4 * step]
                nc.scalar.copy(interleaved(run), by_lines(g_planes[e][:, :, s : s + step]))
                nc.vector.quantize_mx(out=words[:, s : s + step].bitcast(E5M2), scales=scales[:, s : s + step], in_=run)
            g_codes[e] = (words, scales)

        order = [(g, s) for g in range(NG) for s in range(SB)]

        def first_product(e):
            words, scales = g_codes[e]
            for g, s in order:
                bank = pa.tile([P, 512], F32, name="dh_bank")
                nc.tensor.matmul_mx(
                    out=bank[:],
                    lhsT=words[:, P * s : P * s + P].bitcast(E5M2),
                    lhsT_scale=scales[:, P * s : P * s + P],
                    rhs=w2_w[e][:, 1024 * g : 1024 * g + 1024].bitcast(E2M1),
                    rhs_scale=w2_sc[:, e, 512 * g : 512 * g + 512],
                    start=True,
                    stop=True,
                )
                dht = turn.tile([P, X4, P], F32, name="dht")
                nc.scalar.copy(dht[:], bank[:].rearrange("p (m t) -> p t m", t=X4))
                turned_in[e, g, s] = dht
                kept = a_tiles[1, e, g][:, :, P * s : P * (s + 1)]
                nc.scalar.activation(kept, kept, ACT.Relu)
                if s == SB - 1:
                    steps_1[e, g] = ring.tile([P, X4 * C], BF16, name="mask", bufs=3, align_bytes=64)
                    nc.scalar.activation(interleaved(steps_1[e, g][:]), by_lines(a_tiles[1, e, g][:]), ACT.Sign)

        def hidden(e, between):
            d1 = [ring.tile([P, X4 * C], BF16, name=f"d1_{g}", align_bytes=64, bufs=1) for g in range(NG)]
            d3 = [ring.tile([P, X4 * C], BF16, name=f"d3_{g}", align_bytes=64, bufs=1) for g in range(NG)]
            for n, (g, s) in enumerate(order):
                cols = slice(P * s, P * s + P)
                run = slice(X4 * P * s, X4 * P * (s + 1))
                dht = turned_in[e, g, s]
                bank = pb.tile([P, X4, P], F32, name="turned")
                for t in range(X4):
                    nc.tensor.transpose(bank[:, t, :], dht[:, t, :], ident[:])
                for d, which in ((d3, 1), (d1, 3)):
                    nc.vector.tensor_tensor(
                        interleaved(d[g][:, run]), by_lines(bank[:]), by_lines(a_tiles[which, e, g][:, :, cols]), ALU.mult
                    )
                between(n, d1, d3)

        codes = {}

        def close_half(e, g, d1, d3):
            nc.vector.tensor_tensor(d1[g][:], d1[g][:], steps_1[e, g][:], ALU.mult)
            quantise_hidden(3, e, g, d3[g])
            quantise_hidden(1, e, g, d1[g])

        def quantise_hidden(which, e, g, d):
            words = ring.tile([P, C], U32, name=f"d_words{which}{g}", align_bytes=64)
            scales = ring.tile([P, C], U8, name=f"d_scales{which}{g}", align_bytes=64)
            nc.vector.quantize_mx(out=words[:].bitcast(E5M2), scales=scales[:], in_=d[:])
            codes[which, e, g] = (words, scales)

        def second_product(e):
            for kb in range(KB):
                bank = pc.tile([P, C], F32, name=f"dx_bank{kb}")
                passes = [(which, g) for g in range(NG) for which in (3, 1)]
                for n, (which, g) in enumerate(passes):
                    w, sc = (w1_w, w1_sc) if which == 1 else (w3_w, w3_sc)
                    words, scales = codes[which, e, g]
                    nc.tensor.matmul_mx(
                        out=bank[:],
                        lhsT=w[:, NG * e + g, 2 * P * kb : 2 * P * (kb + 1)].bitcast(E2M1),
                        lhsT_scale=sc[:, NG * e + g, P * kb : P * (kb + 1)],
                        rhs=words[:].bitcast(E5M2),
                        rhs_scale=scales[:],
                        start=(n == 0),
                        stop=(n == len(passes) - 1),
                    )
                nc.scalar.copy(dx[kb][:, C * e : C * (e + 1)], bank[:])

        gather(0)
        quantise_g(0, 128)
        first_product(0)
        gather(1)
        for e in range(E):

            def between(n, d1, d3):
                if n == 1 and e + 1 < E:
                    quantise_g(e + 1, 256)
                    first_product(e + 1)
                if n == 4:
                    close_half(e, 0, d1, d3)
                if n == 7:
                    close_half(e, 1, d1, d3)

            hidden(e, between)
            if e + 2 < E:
                for g in range(NG):
                    load_a(1, e + 2, g)
                    load_a(3, e + 2, g)
                gather(e + 2)
            second_product(e)

        for kb in range(KB):
            half = T // (kb + 1)
            picks = ring.tile([P, X4, C], F32, name="g4")
            flat = picks[:].rearrange("p t c -> p (t c)")
            first, second = flat[:, 0:T], flat[:, T : 2 * T]
            total = ring.tile([P, T], F32, name="total", bufs=1)
            for h in range(0, T, half):
                span = slice(h, h + half)
                lists = slice(h // 16, (h + half) // 16)
                nc.vector.tensor_copy(first[:, span], dx[kb][:].indirect(pos1_sb[:, lists]))
                nc.vector.tensor_copy(second[:, span], dx[kb][:].indirect(pos2_sb[:, lists]))
                engine = nc.gpsimd if kb == 0 else nc.vector
                engine.tensor_tensor(total[:, span], first[:, span], second[:, span], ALU.add)
                nc.sync.dma_start(out[P * kb : P * (kb + 1), span], total[:, span])
